import numpy as np
import ml_dtypes


def mxq(x, axis, fmt="e4m3"):
    dtype, down = {"e4m3": (ml_dtypes.float8_e4m3fn, 7), "e5m2": (ml_dtypes.float8_e5m2, 14)}[fmt]
    v = np.moveaxis(np.asarray(x, np.float32).astype(ml_dtypes.bfloat16).astype(np.float64), axis, -1)
    blocks = v.reshape(v.shape[:-1] + (-1, 32))
    amax = np.abs(blocks).max(-1, keepdims=True)
    byte = np.maximum(np.where(amax > 0, np.frexp(amax)[1] - 1 + 127, 0) - down, 1)
    scale = np.exp2(byte - 127.0)
    codes = (blocks / scale).astype(np.float32).astype(dtype).astype(np.float64)
    return np.moveaxis((codes * scale).reshape(v.shape), -1, axis)


WIDE = False


def mx_kscale(k):
    if not WIDE:
        return np.ones(k)
    levels = np.array([10, -10, 5, -5, 0])
    if k % 512:
        return np.exp2(np.random.permutation(np.resize(levels, k // 32))).repeat(32)
    a = np.empty((k // 512, 16))
    for p in range(k // 512):
        a[p, :8] = np.random.permutation(np.resize(levels, 8))
        for g in range(8):
            far = levels[np.abs(levels - a[p, g]) >= 10]
            a[p, g + 8] = far[np.random.randint(len(far))]
    return np.exp2(a.ravel()).repeat(32)


def f64(x):
    return np.asarray(x).astype(np.float64)


def striped(idx):
    return np.tile(idx.reshape(-1, 16).T, (8, 1)).astype(np.uint16)


def unstriped(offs):
    return offs[:16].T.reshape(-1).astype(np.int64)


def striped8(idx):
    return np.concatenate([x.reshape(-1, 16).T for x in idx]).astype(np.uint16)


def runs(offs, k):
    lists = np.stack([offs[16 * r : 16 * r + 16].T.reshape(-1) for r in range(8)]).astype(np.int64)
    return lists[np.arange(k) % 512 // 64]


def pack_weight(w):
    k, n = w.shape
    w = f64(np.asarray(w, np.float32).astype(ml_dtypes.bfloat16)).reshape(k // 32, 32, n)
    amax = np.abs(w).max(1)
    byte = np.clip(np.where(amax > 0, np.frexp(amax)[1] - 1 + 127 - 7, 1), 1, 254)
    scaled = (w * np.exp2(127.0 - byte)[:, None, :]).reshape(k, n).astype(np.float32)
    words = np.ascontiguousarray(scaled.reshape(k // 512, 128, 4, n).transpose(0, 1, 3, 2)).astype(ml_dtypes.float8_e4m3fn).view(np.uint8)
    return words, np.ascontiguousarray(byte.astype(np.uint8).reshape(k // 512, 16, n))


def unpack_weight(words, scales):
    g, p, n, _ = words.shape
    vals = np.ascontiguousarray(words).view(ml_dtypes.float8_e4m3fn).astype(np.float64) * np.repeat(np.exp2(scales.astype(np.float64) - 127.0), 8, axis=1)[..., None]
    return vals.transpose(0, 1, 3, 2).reshape(g * 512, n)


E2M1 = np.array([0.0, 0.5, 1.0, 1.5, 2.0, 3.0, 4.0, 6.0, -0.0, -0.5, -1.0, -1.5, -2.0, -3.0, -4.0, -6.0])


def pack_fp4(w):
    k, n = w.shape
    w = f64(np.asarray(w, np.float32).astype(ml_dtypes.bfloat16)).reshape(k // 32, 32, n)
    amax = np.abs(w).max(1)
    mant, ex = np.frexp(amax / 6.0)
    byte = np.clip(np.where(amax > 0, np.where(mant > 0.5, ex, ex - 1) + 127, 1), 1, 254)
    scaled = (w * np.exp2(127.0 - byte)[:, None, :]).reshape(k, n).astype(np.float32)
    c = np.ascontiguousarray(scaled.reshape(k // 512, 128, 4, n).transpose(0, 1, 3, 2)).astype(ml_dtypes.float4_e2m1fn).view(np.uint8) & 0xF
    words = (c[..., 0::2] | (c[..., 1::2] << 4)).reshape(k // 512, 128, 2 * n)
    return np.ascontiguousarray(words), np.ascontiguousarray(byte.astype(np.uint8).reshape(k // 512, 16, n))


def unpack_fp4(words, scales):
    g, _, n = scales.shape
    words = np.ascontiguousarray(words).reshape(g, 128, n, 2)
    nib = np.empty((g, 128, n, 4), np.uint8)
    nib[..., 0::2] = words & 0xF
    nib[..., 1::2] = words >> 4
    vals = E2M1[nib] * np.repeat(np.exp2(scales.astype(np.float64) - 127.0), 8, axis=1)[..., None]
    return vals.transpose(0, 1, 3, 2).reshape(g * 512, n)


def sigmoid(v):
    return 1.0 / (1.0 + np.exp(-np.maximum(v, -700.0)))


K, T, S, N, G, H, W = 512, 1024, 256, 512, 2048, 512, 128


def setup_inputs():
    n = np.random.standard_normal
    s = mx_kscale(K)[:, None]
    u = mx_kscale(K)
    packed_xT = pack_weight(n((K, T)) * s)
    packed_dT = pack_weight(n((K, G)) / s)
    packed_w1 = pack_fp4(n((H, N)) / np.sqrt(H) / u[:, None])
    perm = np.random.permutation(S)
    perm2 = np.random.permutation(S)
    return {
        "x_words": packed_xT[0],
        "x_scales": packed_xT[1],
        "d_words": packed_dT[0],
        "d_scales": packed_dT[1],
        "gn": (np.random.uniform(0.5, 1.5, (H, 1)) * u[:, None]).astype(np.float32),
        "w1_words": packed_w1[0],
        "w1_scales": packed_w1[1],
        "sl": np.random.uniform(1.0, 2.0, (N, 1)).astype(np.float32),
        "th": (0.5 * n((N, 1))).astype(np.float32),
        "offs": striped(np.random.permutation(T)[:S]),
        "k1": striped8(np.random.randint(0, G, (8, H))),
        "hz": striped8(np.random.randint(0, T, (8, S))),
        "k2": striped8(np.random.randint(0, G, (8, H))),
        "hy": striped8(np.random.randint(0, T, (8, S))),
        "k3": striped8(np.random.randint(0, G, (8, H))),
        "n1": striped(perm[:W]),
        "n2": striped(perm[W:]),
        "n3": striped(perm2[:W]),
        "n4": striped(perm2[W:]),
        "n5": striped(np.random.permutation(S)),
        "n6": striped(np.random.permutation(S)),
        "n7": striped(np.random.permutation(S)),
        "n8": striped(np.random.permutation(S)),
    }


def reference(x_words, x_scales, d_words, d_scales, gn, w1_words, w1_scales, sl, th, offs, k1, hz, k2, hy, k3, n1, n2, n3, n4, n5, n6, n7, n8):
    d_k1 = unpack_weight(d_words, d_scales)[np.arange(K)[:, None], runs(k1, K)]
    xq = unpack_weight(x_words, x_scales)[:, unstriped(offs)]
    d_k2 = unpack_weight(d_words, d_scales)[np.arange(K)[:, None], runs(k2, K)]
    x_hz = unpack_weight(x_words, x_scales)[np.arange(K)[:, None], runs(hz, K)]
    d_k3 = unpack_weight(d_words, d_scales)[np.arange(K)[:, None], runs(k3, K)]
    x_hy = unpack_weight(x_words, x_scales)[np.arange(K)[:, None], runs(hy, K)]
    h = 0.0625 * (d_k1.T @ xq + d_k2.T @ x_hz + d_k3.T @ x_hy)
    pa = h[:, unstriped(n1)]
    pb = h[:, unstriped(n2)]
    rb = pa + pb
    ra = np.minimum(pa, pb)
    ua = np.zeros((H, S))
    ua[:, unstriped(n3)] = ra
    ub = ua.copy()
    ub[:, unstriped(n4)] = rb
    ds = np.zeros((H, S))
    ds[:, unstriped(n5)] = ub
    z = f64(gn) * (ub - ds)
    h2 = unpack_fp4(w1_words, w1_scales).T @ mxq(z, 0, "e4m3")
    ds3 = np.zeros((N, S))
    ds3[:, unstriped(n7)] = h2
    ds2 = np.zeros((N, S))
    ds2[:, unstriped(n6)] = h2
    sg = sigmoid(f64(sl) * (ds2[:, unstriped(n8)] - f64(th)))
    return ds3 * sg

@@ -1,0 +1,259 @@
+from contextlib import ExitStack
+
+import concourse.mybir as mybir
+from concourse.masks import make_identity
+
+F32 = mybir.dt.float32
+BF16 = mybir.dt.bfloat16
+I32 = mybir.dt.int32
+U32 = mybir.dt.uint32
+U16 = mybir.dt.uint16
+U8 = mybir.dt.uint8
+FP8X4 = mybir.dt.float8_e4m3fn_x4
+FP4X4 = mybir.dt.float4_e2m1fn_x4
+ALU = mybir.AluOpType
+ACT = mybir.ActivationFunctionType
+
+K, T, S, N, G, H, W = 512, 1024, 256, 512, 2048, 512, 128
+P = 128
+TILES = H // P
+HALF = H // 2
+SCATTER_WINDOW = 384
+SIGMOID_WINDOW = 512
+ALIGN = 64
+
+FLOPS = 2 * 3 * K * H * S + 2 * H * N * S
+
+
+def tile_picked_mthhzncpsdesntw_none_p_kernel(
+    tc, x_words, x_scales, d_words, d_scales, gn, w1_words, w1_scales, sl, th,
+    offs, k1, hz, k2, hy, k3, n1, n2, n3, n4, n5, n6, n7, n8, out,
+):
+    nc = tc.nc
+    with ExitStack() as ctx:
+        lists = ctx.enter_context(tc.tile_pool(name="lists", bufs=1))
+        sb = ctx.enter_context(tc.tile_pool(name="sb", bufs=1))
+        psum = ctx.enter_context(tc.psum_pool(name="psum", bufs=1))
+
+        def tile(shape, dtype, name, tag=None):
+            return sb.tile(shape, dtype, name=name, tag=tag or name, align_bytes=ALIGN)
+
+        def load_list(src, name):
+            held = lists.tile(list(src.shape), U16, name=name)
+            nc.sync.dma_start(held[:], src)
+            return held
+
+        def load_rows(src, name, tag=None):
+            held = tile([P, TILES], F32, name, tag)
+            with nc.allow_non_contiguous_dma(reason="one value a partition and row tile"):
+                nc.sync.dma_start(held[:], src.rearrange("(u p) o -> p (u o)", p=P))
+            return held
+
+        def gather(dst, table, offsets):
+            nc.vector.tensor_copy(dst, table[:].indirect(offsets))
+
+        def place_scale_rows(queue, plane, gathered):
+            for q in range(4):
+                queue.dma_start(plane[32 * q : 32 * q + 4, :].bitcast(I32), gathered[32 * q : 32 * q + 32 : 8, :].bitcast(I32))
+
+        xs_table = tile([P, T], U8, "xs_table")
+        ds_table = tile([P, G], U8, "ds_table")
+        nc.vector.memset(xs_table[:].bitcast(I32), 0)
+        nc.vector.memset(ds_table[:].bitcast(I32), 0)
+        nc.scalar.dma_start(xs_table[0:P:8, :].bitcast(I32), x_scales[0].bitcast(I32))
+        nc.scalar.dma_start(ds_table[0:P:8, :].bitcast(I32), d_scales[0].bitcast(I32))
+        x_lists = [load_list(offs, "offs"), load_list(hz, "hz"), load_list(hy, "hy")]
+        d_lists = [load_list(k1, "k1")]
+        dw_table = tile([P, G], U32, "dw_table")
+        xw_table = tile([P, T], U32, "xw_table")
+        nc.sync.dma_start(dw_table[:].bitcast(I32), d_words[0].rearrange("p c r -> p (c r)").bitcast(I32))
+        nc.sync.dma_start(xw_table[:].bitcast(I32), x_words[0].rearrange("p c r -> p (c r)").bitcast(I32))
+        d_lists.extend([load_list(k2, "k2"), load_list(k3, "k3")])
+        n1_list, n2_list = load_list(n1, "n1"), load_list(n2, "n2")
+        n3_list, n4_list = load_list(n3, "n3"), load_list(n4, "n4")
+        n5_list = load_list(n5, "n5")
+        gain = load_rows(gn, "gain")
+        n6_list, n7_list, n8_list = load_list(n6, "n6"), load_list(n7, "n7"), load_list(n8, "n8")
+
+        planes = [tile([P, 3 * S + 3 * HALF], U8, "plane0"), tile([P, 3 * HALF], U8, "plane1")]
+        for plane in planes:
+            nc.gpsimd.memset(plane[:].bitcast(I32), 0)
+        ident = tile([P, P], F32, "ident")
+        make_identity(nc, ident[:])
+
+        def d_offsets(i, half):
+            return d_lists[i][:, half * HALF // 16 : (half + 1) * HALF // 16]
+
+        bytes0 = tile([P, 3 * S + 3 * HALF], U8, "bytes0")
+        for i in range(3):
+            gather(bytes0[:, i * S : (i + 1) * S], xs_table, x_lists[i][:])
+        for i in range(3):
+            gather(bytes0[:, 3 * S + i * HALF : 3 * S + (i + 1) * HALF], ds_table, d_offsets(i, 0))
+        place_scale_rows(nc.scalar, planes[0], bytes0)
+        d_codes = {}
+        for i in range(3):
+            d_codes[i, 0] = tile([P, HALF], U32, f"d_codes{i}0")
+            gather(d_codes[i, 0][:], dw_table, d_offsets(i, 0))
+        x_codes = []
+        for i in range(3):
+            x_codes.append(tile([P, S], U32, f"x_codes{i}"))
+            gather(x_codes[i][:], xw_table, x_lists[i][:])
+
+        def first_products(half):
+            banks = [psum.tile([P, S], F32, name=f"h_bank{half}{v}", tag="acc", bufs=3) for v in range(2)]
+            base = 3 * S if half == 0 else 0
+            for i in range(3):
+                for v in range(2):
+                    at = base + i * HALF + v * P
+                    nc.tensor.matmul_mx(
+                        out=banks[v][:],
+                        lhsT=d_codes[i, half][:, v * P : (v + 1) * P].bitcast(FP8X4),
+                        lhsT_scale=planes[half][:, at : at + P],
+                        rhs=x_codes[i][:].bitcast(FP8X4),
+                        rhs_scale=planes[0][:, i * S : (i + 1) * S],
+                        start=(i == 0),
+                        stop=(i == 2),
+                    )
+            return banks
+
+        h, pa, pb, ub, ubg, ubg_t = {}, {}, {}, {}, {}, {}
+        z_t = [tile([P, 2, 2 * P], BF16, f"z_t{c}") for c in range(2)]
+
+        def fetch_pairs(u):
+            pa[u] = tile([P, W], F32, f"pa{u}")
+            pb[u] = tile([P, W], F32, f"pb{u}")
+            nc.scalar.activation(pa[u][:], h[u][:].indirect(n1_list[:]), ACT.Copy)
+            nc.scalar.activation(pb[u][:], h[u][:].indirect(n2_list[:]), ACT.Copy)
+
+        ra, rb = {}, {}
+
+        def combine_pairs(u):
+            ra[u] = tile([P, W], F32, f"ra{u}")
+            rb[u] = tile([P, W], F32, f"rb{u}")
+            nc.vector.tensor_tensor(ra[u][:], pa[u][:], pb[u][:], ALU.min)
+            nc.vector.tensor_tensor(rb[u][:], pa[u][:], pb[u][:], ALU.add)
+
+        def share_out(u):
+            ub[u] = tile([P, S], F32, f"ub{u}")
+            nc.scalar.activation(ub[u][:].indirect(n3_list[:]), ra[u][:], ACT.Copy)
+            nc.scalar.activation(ub[u][:].indirect(n4_list[:]), rb[u][:], ACT.Copy)
+            ubg[u] = tile([P, S], F32, f"ubg{u}")
+            nc.vector.tensor_scalar(ubg[u][:], ub[u][:], gain[:, u : u + 1], None, ALU.mult)
+            bank = psum.tile([P, 2, P], F32, name=f"ubg_bank{u}", tag="ubg_bank", bufs=1)
+            for c in range(2):
+                nc.tensor.transpose(bank[:, c, :], ubg[u][:, c * P : (c + 1) * P], ident[:])
+            ubg_t[u] = tile([P, 2, 2, 32, 2], F32, f"ubg_t{u}")
+            nc.vector.tensor_copy(ubg_t[u][:], bank[:].rearrange("j c (q e b) -> j c e q b", e=2, b=2))
+
+        def send_and_subtract(u):
+            dsg = tile([P, SCATTER_WINDOW], F32, f"dsg{u}")
+            nc.scalar.activation(dsg[:].indirect(n5_list[:]), ubg[u][:], ACT.Copy)
+            bank = psum.tile([P, 2, P], F32, name=f"dsg_bank{u}", tag="dsg_bank", bufs=2)
+            for c in range(2):
+                nc.tensor.transpose(bank[:, c, :], dsg[:, c * P : (c + 1) * P], ident[:])
+            for c in range(2):
+                nc.vector.tensor_tensor(
+                    z_t[c][:, :, 64 * u : 64 * (u + 1)].rearrange("j e (q b) -> j e q b", b=2),
+                    ubg_t[u][:, c],
+                    bank[:, c, :].rearrange("j (q e b) -> j e q b", e=2, b=2),
+                    ALU.subtract,
+                )
+
+        banks = first_products(0)
+        bytes1 = tile([P, 3 * HALF], U8, "bytes1", tag="xw_table")
+        for i in range(3):
+            gather(bytes1[:, i * HALF : (i + 1) * HALF], ds_table, d_offsets(i, 1))
+        place_scale_rows(nc.sync, planes[1], bytes1)
+        for u in range(2):
+            h[u] = tile([P, S], F32, f"h{u}")
+            nc.scalar.activation(h[u][:], banks[u][:], ACT.Copy, scale=0.0625)
+            fetch_pairs(u)
+        for u in range(2):
+            combine_pairs(u)
+        for i, after in enumerate(("pa0", "pb0", "pa1")):
+            d_codes[i, 1] = tile([P, HALF], U32, f"d_codes{i}1", tag=after)
+            gather(d_codes[i, 1][:], dw_table, d_offsets(i, 1))
+        banks = first_products(1)
+        for u in range(2, 4):
+            h[u] = tile([P, S], F32, f"h{u}")
+            nc.vector.tensor_scalar(h[u][:], banks[u - 2][:], 0.0625, None, ALU.mult)
+
+        slope = load_rows(sl, "slope", tag="ds_table")
+        threshold = load_rows(th, "threshold", tag="bytes0")
+        bias = tile([P, TILES], F32, "bias")
+        nc.vector.scalar_tensor_tensor(bias[:], slope[:], -1.0, threshold[:], ALU.mult, ALU.mult)
+        w1_codes = tile([P, 2 * N], U8, "w1_codes", tag="dw_table")
+        nc.sync.dma_start(w1_codes[:].bitcast(I32), w1_words[0].bitcast(I32))
+        w1_plane = tile([P, N], U8, "w1_plane", tag="xw_table")
+        nc.vector.memset(w1_plane[:].bitcast(I32), 0)
+        for q in range(4):
+            nc.sync.dma_start(w1_plane[32 * q : 32 * q + 4, :].bitcast(I32), w1_scales[0, 4 * q : 4 * q + 4, :].bitcast(I32))
+
+        share_out(0)
+        share_out(1)
+        send_and_subtract(0)
+        fetch_pairs(2)
+        combine_pairs(2)
+        send_and_subtract(1)
+        fetch_pairs(3)
+        combine_pairs(3)
+        share_out(2)
+        share_out(3)
+        send_and_subtract(2)
+        send_and_subtract(3)
+
+        z_codes = tile([P, S], U32, "z_codes")
+        z_plane = tile([P, S], U8, "z_plane")
+        grouped = []
+        for c, engine_copy in enumerate((nc.scalar.copy, nc.vector.tensor_copy)):
+            bank = psum.tile([P, 2, P], F32, name=f"z_bank{c}", tag="z_bank", bufs=2)
+            for e in range(2):
+                nc.tensor.transpose(bank[:, e, :], z_t[c][:, e, :].bitcast(F32), ident[:])
+            grouped.append(tile([P, P, 2], F32, f"grouped{c}"))
+            engine_copy(grouped[c][:], bank[:].rearrange("p e j -> p j e"))
+        for c in range(2):
+            nc.vector.quantize_mx(
+                out=z_codes[:, c * P : (c + 1) * P].bitcast(FP8X4),
+                scales=z_plane[:, c * P : (c + 1) * P],
+                in_=grouped[c][:].rearrange("p j e -> p (j e)").bitcast(BF16),
+            )
+
+        def second_product(m, cols):
+            bank = psum.tile([P, cols.stop - cols.start], F32, name=f"h2_bank{m}_{cols.start}", tag="acc", bufs=3)
+            nc.tensor.matmul_mx(
+                out=bank[:],
+                lhsT=w1_codes[:, 2 * P * m : 2 * P * (m + 1)].bitcast(FP4X4),
+                lhsT_scale=w1_plane[:, P * m : P * (m + 1)],
+                rhs=z_codes[:, cols].bitcast(FP8X4),
+                rhs_scale=z_plane[:, cols],
+                start=True,
+                stop=True,
+            )
+            return bank
+
+        halves = [slice(0, P), slice(P, S)]
+        whole = [slice(0, S)]
+        for m in range(TILES):
+            h2 = tile([P, S], F32, f"h2_{m}")
+            ds2 = tile([P, SIGMOID_WINDOW], F32, f"ds2_{m}")
+            ds3 = tile([P, SCATTER_WINDOW], F32, f"ds3_{m}")
+            sg = tile([P, S], F32, f"sg{m}")
+            result = tile([P, S], F32, f"result{m}")
+            for cols in halves if m == 0 else whole:
+                bank = second_product(m, cols)
+                if m == 0 and cols.start == 0:
+                    nc.scalar.copy(h2[:, cols], bank[:])
+                else:
+                    nc.vector.tensor_copy(h2[:, cols], bank[:])
+                nc.scalar.activation(ds2[:].indirect(n6_list[:, cols.start // 16 : cols.stop // 16]), h2[:, cols], ACT.Copy)
+            nc.scalar.activation(ds3[:].indirect(n7_list[:]), h2[:], ACT.Copy)
+            for cols in halves if m == TILES - 1 else whole:
+                nc.scalar.activation(
+                    sg[:, cols],
+                    ds2[:].indirect(n8_list[:, cols.start // 16 : cols.stop // 16]),
+                    ACT.Sigmoid,
+                    bias=bias[:, m : m + 1],
+                    scale=slope[:, m : m + 1],
+                )
+                nc.vector.tensor_tensor(result[:, cols], ds3[:, cols], sg[:, cols], ALU.mult)
+                nc.sync.dma_start(out[m * P : (m + 1) * P, cols], result[:, cols])

@@ -58,17 +58,17 @@ def tile_picked_mthhzncpsdesntw_none_p_kernel(
 
         xs_table = tile([P, T], U8, "xs_table")
         ds_table = tile([P, G], U8, "ds_table")
-        nc.vector.memset(xs_table[:].bitcast(I32), 0)
-        nc.vector.memset(ds_table[:].bitcast(I32), 0)
-        nc.scalar.dma_start(xs_table[0:P:8, :].bitcast(I32), x_scales[0].bitcast(I32))
-        nc.scalar.dma_start(ds_table[0:P:8, :].bitcast(I32), d_scales[0].bitcast(I32))
-        x_lists = [load_list(offs, "offs"), load_list(hz, "hz"), load_list(hy, "hy")]
-        d_lists = [load_list(k1, "k1")]
+        nc.gpsimd.memset(xs_table[:].bitcast(I32), 0)
+        nc.gpsimd.memset(ds_table[:].bitcast(I32), 0)
+        nc.sync.dma_start(xs_table[0:P:8, :].bitcast(I32), x_scales[0].bitcast(I32))
+        x_lists = [load_list(offs, "offs")]
+        nc.sync.dma_start(ds_table[0:P:8, :].bitcast(I32), d_scales[0].bitcast(I32))
+        x_lists.extend([load_list(hz, "hz"), load_list(hy, "hy")])
+        d_lists = [load_list(k1, "k1"), load_list(k2, "k2"), load_list(k3, "k3")]
         dw_table = tile([P, G], U32, "dw_table")
         xw_table = tile([P, T], U32, "xw_table")
-        nc.sync.dma_start(dw_table[:].bitcast(I32), d_words[0].rearrange("p c r -> p (c r)").bitcast(I32))
         nc.sync.dma_start(xw_table[:].bitcast(I32), x_words[0].rearrange("p c r -> p (c r)").bitcast(I32))
-        d_lists.extend([load_list(k2, "k2"), load_list(k3, "k3")])
+        nc.sync.dma_start(dw_table[:].bitcast(I32), d_words[0].rearrange("p c r -> p (c r)").bitcast(I32))
         n1_list, n2_list = load_list(n1, "n1"), load_list(n2, "n2")
         n3_list, n4_list = load_list(n3, "n3"), load_list(n4, "n4")
         n5_list = load_list(n5, "n5")
@@ -90,20 +90,22 @@ def tile_picked_mthhzncpsdesntw_none_p_kernel(
         for i in range(3):
             gather(bytes0[:, 3 * S + i * HALF : 3 * S + (i + 1) * HALF], ds_table, d_offsets(i, 0))
         place_scale_rows(nc.scalar, planes[0], bytes0)
-        d_codes = {}
-        for i in range(3):
-            d_codes[i, 0] = tile([P, HALF], U32, f"d_codes{i}0")
-            gather(d_codes[i, 0][:], dw_table, d_offsets(i, 0))
         x_codes = []
         for i in range(3):
             x_codes.append(tile([P, S], U32, f"x_codes{i}"))
             gather(x_codes[i][:], xw_table, x_lists[i][:])
+        d_codes = {}
+        for i in range(3):
+            d_codes[i, 0] = tile([P, HALF], U32, f"d_codes{i}0")
+            gather(d_codes[i, 0][:], dw_table, d_offsets(i, 0))
+
+        bank_tags = (("acc0", "acc1"), ("ubg_bank", "dsg_bank"))
 
         def first_products(half):
-            banks = [psum.tile([P, S], F32, name=f"h_bank{half}{v}", tag="acc", bufs=3) for v in range(2)]
+            banks = [psum.tile([P, S], F32, name=f"h_bank{half}{v}", tag=bank_tags[half][v]) for v in range(2)]
             base = 3 * S if half == 0 else 0
-            for i in range(3):
-                for v in range(2):
+            for v in range(2):
+                for i in range(3):
                     at = base + i * HALF + v * P
                     nc.tensor.matmul_mx(
                         out=banks[v][:],
@@ -128,18 +130,25 @@ def tile_picked_mthhzncpsdesntw_none_p_kernel(
         ra, rb = {}, {}
 
         def combine_pairs(u):
-            ra[u] = tile([P, W], F32, f"ra{u}")
-            rb[u] = tile([P, W], F32, f"rb{u}")
-            nc.vector.tensor_tensor(ra[u][:], pa[u][:], pb[u][:], ALU.min)
-            nc.vector.tensor_tensor(rb[u][:], pa[u][:], pb[u][:], ALU.add)
+            for v in (u, u + 1):
+                ra[v] = tile([P, W], F32, f"ra{v}")
+                nc.vector.tensor_tensor(ra[v][:], pa[v][:], pb[v][:], ALU.min)
+            for v in (u, u + 1):
+                rb[v] = tile([P, W], F32, f"rb{v}", tag=f"h{u + 1}" if v == u else None)
+                nc.vector.tensor_tensor(rb[v][:], pa[v][:], pb[v][:], ALU.add)
 
         def share_out(u):
-            ub[u] = tile([P, S], F32, f"ub{u}")
-            nc.scalar.activation(ub[u][:].indirect(n3_list[:]), ra[u][:], ACT.Copy)
-            nc.scalar.activation(ub[u][:].indirect(n4_list[:]), rb[u][:], ACT.Copy)
+            for v in (u, u + 1):
+                ub[v] = tile([P, S], F32, f"ub{v}")
+                nc.scalar.activation(ub[v][:].indirect(n3_list[:]), ra[v][:], ACT.Copy)
+            for v in (u, u + 1):
+                nc.scalar.activation(ub[v][:].indirect(n4_list[:]), rb[v][:], ACT.Copy)
+                apply_gain(v)
+
+        def apply_gain(u):
             ubg[u] = tile([P, S], F32, f"ubg{u}")
             nc.vector.tensor_scalar(ubg[u][:], ub[u][:], gain[:, u : u + 1], None, ALU.mult)
-            bank = psum.tile([P, 2, P], F32, name=f"ubg_bank{u}", tag="ubg_bank", bufs=1)
+            bank = psum.tile([P, 2, P], F32, name=f"ubg_bank{u}", tag="ubg_bank")
             for c in range(2):
                 nc.tensor.transpose(bank[:, c, :], ubg[u][:, c * P : (c + 1) * P], ident[:])
             ubg_t[u] = tile([P, 2, 2, 32, 2], F32, f"ubg_t{u}")
@@ -148,7 +157,7 @@ def tile_picked_mthhzncpsdesntw_none_p_kernel(
         def send_and_subtract(u):
             dsg = tile([P, SCATTER_WINDOW], F32, f"dsg{u}")
             nc.scalar.activation(dsg[:].indirect(n5_list[:]), ubg[u][:], ACT.Copy)
-            bank = psum.tile([P, 2, P], F32, name=f"dsg_bank{u}", tag="dsg_bank", bufs=2)
+            bank = psum.tile([P, 2, P], F32, name=f"dsg_bank{u}", tag="dsg_bank")
             for c in range(2):
                 nc.tensor.transpose(bank[:, c, :], dsg[:, c * P : (c + 1) * P], ident[:])
             for c in range(2):
@@ -160,7 +169,7 @@ def tile_picked_mthhzncpsdesntw_none_p_kernel(
                 )
 
         banks = first_products(0)
-        bytes1 = tile([P, 3 * HALF], U8, "bytes1", tag="xw_table")
+        bytes1 = tile([P, 3 * HALF], U8, "bytes1", tag="d_codes00")
         for i in range(3):
             gather(bytes1[:, i * HALF : (i + 1) * HALF], ds_table, d_offsets(i, 1))
         place_scale_rows(nc.sync, planes[1], bytes1)
@@ -168,8 +177,7 @@ def tile_picked_mthhzncpsdesntw_none_p_kernel(
             h[u] = tile([P, S], F32, f"h{u}")
             nc.scalar.activation(h[u][:], banks[u][:], ACT.Copy, scale=0.0625)
             fetch_pairs(u)
-        for u in range(2):
-            combine_pairs(u)
+        combine_pairs(0)
         for i, after in enumerate(("pa0", "pb0", "pa1")):
             d_codes[i, 1] = tile([P, HALF], U32, f"d_codes{i}1", tag=after)
             gather(d_codes[i, 1][:], dw_table, d_offsets(i, 1))
@@ -184,33 +192,30 @@ def tile_picked_mthhzncpsdesntw_none_p_kernel(
         nc.vector.scalar_tensor_tensor(bias[:], slope[:], -1.0, threshold[:], ALU.mult, ALU.mult)
         w1_codes = tile([P, 2 * N], U8, "w1_codes", tag="dw_table")
         nc.sync.dma_start(w1_codes[:].bitcast(I32), w1_words[0].bitcast(I32))
-        w1_plane = tile([P, N], U8, "w1_plane", tag="xw_table")
+        w1_plane = tile([P, N], U8, "w1_plane", tag="d_codes00")
         nc.vector.memset(w1_plane[:].bitcast(I32), 0)
         for q in range(4):
             nc.sync.dma_start(w1_plane[32 * q : 32 * q + 4, :].bitcast(I32), w1_scales[0, 4 * q : 4 * q + 4, :].bitcast(I32))
 
         share_out(0)
-        share_out(1)
         send_and_subtract(0)
         fetch_pairs(2)
+        fetch_pairs(3)
         combine_pairs(2)
         send_and_subtract(1)
-        fetch_pairs(3)
-        combine_pairs(3)
         share_out(2)
-        share_out(3)
         send_and_subtract(2)
         send_and_subtract(3)
 
         z_codes = tile([P, S], U32, "z_codes")
         z_plane = tile([P, S], U8, "z_plane")
         grouped = []
-        for c, engine_copy in enumerate((nc.scalar.copy, nc.vector.tensor_copy)):
+        for c in range(2):
             bank = psum.tile([P, 2, P], F32, name=f"z_bank{c}", tag="z_bank", bufs=2)
             for e in range(2):
                 nc.tensor.transpose(bank[:, e, :], z_t[c][:, e, :].bitcast(F32), ident[:])
             grouped.append(tile([P, P, 2], F32, f"grouped{c}"))
-            engine_copy(grouped[c][:], bank[:].rearrange("p e j -> p j e"))
+            nc.scalar.copy(grouped[c][:], bank[:].rearrange("p e j -> p j e"))
         for c in range(2):
             nc.vector.quantize_mx(
                 out=z_codes[:, c * P : (c + 1) * P].bitcast(FP8X4),
@@ -219,7 +224,7 @@ def tile_picked_mthhzncpsdesntw_none_p_kernel(
             )
 
         def second_product(m, cols):
-            bank = psum.tile([P, cols.stop - cols.start], F32, name=f"h2_bank{m}_{cols.start}", tag="acc", bufs=3)
+            bank = psum.tile([P, cols.stop - cols.start], F32, name=f"h2_bank{m}_{cols.start}", tag="h2_bank", bufs=2)
             nc.tensor.matmul_mx(
                 out=bank[:],
                 lhsT=w1_codes[:, 2 * P * m : 2 * P * (m + 1)].bitcast(FP4X4),
@@ -246,7 +251,7 @@ def tile_picked_mthhzncpsdesntw_none_p_kernel(
                 else:
                     nc.vector.tensor_copy(h2[:, cols], bank[:])
                 nc.scalar.activation(ds2[:].indirect(n6_list[:, cols.start // 16 : cols.stop // 16]), h2[:, cols], ACT.Copy)
-            nc.scalar.activation(ds3[:].indirect(n7_list[:]), h2[:], ACT.Copy)
+                nc.scalar.activation(ds3[:].indirect(n7_list[:, cols.start // 16 : cols.stop // 16]), h2[:, cols], ACT.Copy)
             for cols in halves if m == TILES - 1 else whole:
                 nc.scalar.activation(
                     sg[:, cols],

@@ -80,6 +80,8 @@ def tile_picked_mthhzncpsdesntw_none_p_kernel(
             nc.gpsimd.memset(plane[:].bitcast(I32), 0)
         ident = tile([P, P], F32, "ident")
         make_identity(nc, ident[:])
+        warm = tile([P, 1], F32, "warm")
+        nc.scalar.activation(warm[:], ident[:, 0:1], ACT.Sigmoid)
 
         def d_offsets(i, half):
             return d_lists[i][:, half * HALF // 16 : (half + 1) * HALF // 16]

from contextlib import ExitStack

import concourse.mybir as mybir
from concourse.masks import make_identity

F32 = mybir.dt.float32
BF16 = mybir.dt.bfloat16
I32 = mybir.dt.int32
U32 = mybir.dt.uint32
U16 = mybir.dt.uint16
U8 = mybir.dt.uint8
FP8X4 = mybir.dt.float8_e4m3fn_x4
FP4X4 = mybir.dt.float4_e2m1fn_x4
ALU = mybir.AluOpType
ACT = mybir.ActivationFunctionType

K, T, S, N, G, H, W = 512, 1024, 256, 512, 2048, 512, 128
P = 128
TILES = H // P
HALF = H // 2
SCATTER_WINDOW = 384
SIGMOID_WINDOW = 512
ALIGN = 64

FLOPS = 2 * 3 * K * H * S + 2 * H * N * S


def tile_picked_mthhzncpsdesntw_none_p_kernel(
    tc, x_words, x_scales, d_words, d_scales, gn, w1_words, w1_scales, sl, th,
    offs, k1, hz, k2, hy, k3, n1, n2, n3, n4, n5, n6, n7, n8, out,
):
    nc = tc.nc
    with ExitStack() as ctx:
        lists = ctx.enter_context(tc.tile_pool(name="lists", bufs=1))
        sb = ctx.enter_context(tc.tile_pool(name="sb", bufs=1))
        psum = ctx.enter_context(tc.psum_pool(name="psum", bufs=1))

        def tile(shape, dtype, name, tag=None):
            return sb.tile(shape, dtype, name=name, tag=tag or name, align_bytes=ALIGN)

        def load_list(src, name):
            held = lists.tile(list(src.shape), U16, name=name)
            nc.sync.dma_start(held[:], src)
            return held

        def load_rows(src, name, tag=None):
            held = tile([P, TILES], F32, name, tag)
            with nc.allow_non_contiguous_dma(reason="one value a partition and row tile"):
                nc.sync.dma_start(held[:], src.rearrange("(u p) o -> p (u o)", p=P))
            return held

        def gather(dst, table, offsets):
            nc.vector.tensor_copy(dst, table[:].indirect(offsets))

        def place_scale_rows(queue, plane, gathered):
            for q in range(4):
                queue.dma_start(plane[32 * q : 32 * q + 4, :].bitcast(I32), gathered[32 * q : 32 * q + 32 : 8, :].bitcast(I32))

        xs_table = tile([P, T], U8, "xs_table")
        ds_table = tile([P, G], U8, "ds_table")
        nc.gpsimd.memset(xs_table[:].bitcast(I32), 0)
        nc.gpsimd.memset(ds_table[:].bitcast(I32), 0)
        nc.sync.dma_start(xs_table[0:P:8, :].bitcast(I32), x_scales[0].bitcast(I32))
        x_lists = [load_list(offs, "offs")]
        nc.sync.dma_start(ds_table[0:P:8, :].bitcast(I32), d_scales[0].bitcast(I32))
        x_lists.extend([load_list(hz, "hz"), load_list(hy, "hy")])
        d_lists = [load_list(k1, "k1"), load_list(k2, "k2"), load_list(k3, "k3")]
        dw_table = tile([P, G], U32, "dw_table")
        xw_table = tile([P, T], U32, "xw_table")
        nc.sync.dma_start(xw_table[:].bitcast(I32), x_words[0].rearrange("p c r -> p (c r)").bitcast(I32))
        nc.sync.dma_start(dw_table[:].bitcast(I32), d_words[0].rearrange("p c r -> p (c r)").bitcast(I32))
        n1_list, n2_list = load_list(n1, "n1"), load_list(n2, "n2")
        n3_list, n4_list = load_list(n3, "n3"), load_list(n4, "n4")
        n5_list = load_list(n5, "n5")
        gain = load_rows(gn, "gain")
        n6_list, n7_list, n8_list = load_list(n6, "n6"), load_list(n7, "n7"), load_list(n8, "n8")

        planes = [tile([P, 3 * S + 3 * HALF], U8, "plane0"), tile([P, 3 * HALF], U8, "plane1")]
        for plane in planes:
            nc.gpsimd.memset(plane[:].bitcast(I32), 0)
        ident = tile([P, P], F32, "ident")
        make_identity(nc, ident[:])
        warm = tile([P, 1], F32, "warm")
        nc.scalar.activation(warm[:], ident[:, 0:1], ACT.Sigmoid)

        def d_offsets(i, half):
            return d_lists[i][:, half * HALF // 16 : (half + 1) * HALF // 16]

        bytes0 = tile([P, 3 * S + 3 * HALF], U8, "bytes0")
        for i in range(3):
            gather(bytes0[:, i * S : (i + 1) * S], xs_table, x_lists[i][:])
        for i in range(3):
            gather(bytes0[:, 3 * S + i * HALF : 3 * S + (i + 1) * HALF], ds_table, d_offsets(i, 0))
        place_scale_rows(nc.scalar, planes[0], bytes0)
        x_codes = []
        for i in range(3):
            x_codes.append(tile([P, S], U32, f"x_codes{i}"))
            gather(x_codes[i][:], xw_table, x_lists[i][:])
        d_codes = {}
        for i in range(3):
            d_codes[i, 0] = tile([P, HALF], U32, f"d_codes{i}0")
            gather(d_codes[i, 0][:], dw_table, d_offsets(i, 0))

        bank_tags = (("acc0", "acc1"), ("ubg_bank", "dsg_bank"))

        def first_products(half):
            banks = [psum.tile([P, S], F32, name=f"h_bank{half}{v}", tag=bank_tags[half][v]) for v in range(2)]
            base = 3 * S if half == 0 else 0
            for v in range(2):
                for i in range(3):
                    at = base + i * HALF + v * P
                    nc.tensor.matmul_mx(
                        out=banks[v][:],
                        lhsT=d_codes[i, half][:, v * P : (v + 1) * P].bitcast(FP8X4),
                        lhsT_scale=planes[half][:, at : at + P],
                        rhs=x_codes[i][:].bitcast(FP8X4),
                        rhs_scale=planes[0][:, i * S : (i + 1) * S],
                        start=(i == 0),
                        stop=(i == 2),
                    )
            return banks

        h, pa, pb, ub, ubg, ubg_t = {}, {}, {}, {}, {}, {}
        z_t = [tile([P, 2, 2 * P], BF16, f"z_t{c}") for c in range(2)]

        def fetch_pairs(u):
            pa[u] = tile([P, W], F32, f"pa{u}")
            pb[u] = tile([P, W], F32, f"pb{u}")
            nc.scalar.activation(pa[u][:], h[u][:].indirect(n1_list[:]), ACT.Copy)
            nc.scalar.activation(pb[u][:], h[u][:].indirect(n2_list[:]), ACT.Copy)

        ra, rb = {}, {}

        def combine_pairs(u):
            for v in (u, u + 1):
                ra[v] = tile([P, W], F32, f"ra{v}")
                nc.vector.tensor_tensor(ra[v][:], pa[v][:], pb[v][:], ALU.min)
            for v in (u, u + 1):
                rb[v] = tile([P, W], F32, f"rb{v}", tag=f"h{u + 1}" if v == u else None)
                nc.vector.tensor_tensor(rb[v][:], pa[v][:], pb[v][:], ALU.add)

        def share_out(u):
            for v in (u, u + 1):
                ub[v] = tile([P, S], F32, f"ub{v}")
                nc.scalar.activation(ub[v][:].indirect(n3_list[:]), ra[v][:], ACT.Copy)
            for v in (u, u + 1):
                nc.scalar.activation(ub[v][:].indirect(n4_list[:]), rb[v][:], ACT.Copy)
                apply_gain(v)

        def apply_gain(u):
            ubg[u] = tile([P, S], F32, f"ubg{u}")
            nc.vector.tensor_scalar(ubg[u][:], ub[u][:], gain[:, u : u + 1], None, ALU.mult)
            bank = psum.tile([P, 2, P], F32, name=f"ubg_bank{u}", tag="ubg_bank")
            for c in range(2):
                nc.tensor.transpose(bank[:, c, :], ubg[u][:, c * P : (c + 1) * P], ident[:])
            ubg_t[u] = tile([P, 2, 2, 32, 2], F32, f"ubg_t{u}")
            nc.vector.tensor_copy(ubg_t[u][:], bank[:].rearrange("j c (q e b) -> j c e q b", e=2, b=2))

        def send_and_subtract(u):
            dsg = tile([P, SCATTER_WINDOW], F32, f"dsg{u}")
            nc.scalar.activation(dsg[:].indirect(n5_list[:]), ubg[u][:], ACT.Copy)
            bank = psum.tile([P, 2, P], F32, name=f"dsg_bank{u}", tag="dsg_bank")
            for c in range(2):
                nc.tensor.transpose(bank[:, c, :], dsg[:, c * P : (c + 1) * P], ident[:])
            for c in range(2):
                nc.vector.tensor_tensor(
                    z_t[c][:, :, 64 * u : 64 * (u + 1)].rearrange("j e (q b) -> j e q b", b=2),
                    ubg_t[u][:, c],
                    bank[:, c, :].rearrange("j (q e b) -> j e q b", e=2, b=2),
                    ALU.subtract,
                )

        banks = first_products(0)
        bytes1 = tile([P, 3 * HALF], U8, "bytes1", tag="d_codes00")
        for i in range(3):
            gather(bytes1[:, i * HALF : (i + 1) * HALF], ds_table, d_offsets(i, 1))
        place_scale_rows(nc.sync, planes[1], bytes1)
        for u in range(2):
            h[u] = tile([P, S], F32, f"h{u}")
            nc.scalar.activation(h[u][:], banks[u][:], ACT.Copy, scale=0.0625)
            fetch_pairs(u)
        combine_pairs(0)
        for i, after in enumerate(("pa0", "pb0", "pa1")):
            d_codes[i, 1] = tile([P, HALF], U32, f"d_codes{i}1", tag=after)
            gather(d_codes[i, 1][:], dw_table, d_offsets(i, 1))
        banks = first_products(1)
        for u in range(2, 4):
            h[u] = tile([P, S], F32, f"h{u}")
            nc.vector.tensor_scalar(h[u][:], banks[u - 2][:], 0.0625, None, ALU.mult)

        slope = load_rows(sl, "slope", tag="ds_table")
        threshold = load_rows(th, "threshold", tag="bytes0")
        bias = tile([P, TILES], F32, "bias")
        nc.vector.scalar_tensor_tensor(bias[:], slope[:], -1.0, threshold[:], ALU.mult, ALU.mult)
        w1_codes = tile([P, 2 * N], U8, "w1_codes", tag="dw_table")
        nc.sync.dma_start(w1_codes[:].bitcast(I32), w1_words[0].bitcast(I32))
        w1_plane = tile([P, N], U8, "w1_plane", tag="d_codes00")
        nc.vector.memset(w1_plane[:].bitcast(I32), 0)
        for q in range(4):
            nc.sync.dma_start(w1_plane[32 * q : 32 * q + 4, :].bitcast(I32), w1_scales[0, 4 * q : 4 * q + 4, :].bitcast(I32))

        share_out(0)
        send_and_subtract(0)
        fetch_pairs(2)
        fetch_pairs(3)
        combine_pairs(2)
        send_and_subtract(1)
        share_out(2)
        send_and_subtract(2)
        send_and_subtract(3)

        z_codes = tile([P, S], U32, "z_codes")
        z_plane = tile([P, S], U8, "z_plane")
        grouped = []
        for c in range(2):
            bank = psum.tile([P, 2, P], F32, name=f"z_bank{c}", tag="z_bank", bufs=2)
            for e in range(2):
                nc.tensor.transpose(bank[:, e, :], z_t[c][:, e, :].bitcast(F32), ident[:])
            grouped.append(tile([P, P, 2], F32, f"grouped{c}"))
            nc.scalar.copy(grouped[c][:], bank[:].rearrange("p e j -> p j e"))
        for c in range(2):
            nc.vector.quantize_mx(
                out=z_codes[:, c * P : (c + 1) * P].bitcast(FP8X4),
                scales=z_plane[:, c * P : (c + 1) * P],
                in_=grouped[c][:].rearrange("p j e -> p (j e)").bitcast(BF16),
            )

        def second_product(m, cols):
            bank = psum.tile([P, cols.stop - cols.start], F32, name=f"h2_bank{m}_{cols.start}", tag="h2_bank", bufs=2)
            nc.tensor.matmul_mx(
                out=bank[:],
                lhsT=w1_codes[:, 2 * P * m : 2 * P * (m + 1)].bitcast(FP4X4),
                lhsT_scale=w1_plane[:, P * m : P * (m + 1)],
                rhs=z_codes[:, cols].bitcast(FP8X4),
                rhs_scale=z_plane[:, cols],
                start=True,
                stop=True,
            )
            return bank

        halves = [slice(0, P), slice(P, S)]
        whole = [slice(0, S)]
        for m in range(TILES):
            h2 = tile([P, S], F32, f"h2_{m}")
            ds2 = tile([P, SIGMOID_WINDOW], F32, f"ds2_{m}")
            ds3 = tile([P, SCATTER_WINDOW], F32, f"ds3_{m}")
            sg = tile([P, S], F32, f"sg{m}")
            result = tile([P, S], F32, f"result{m}")
            for cols in halves if m == 0 else whole:
                bank = second_product(m, cols)
                if m == 0 and cols.start == 0:
                    nc.scalar.copy(h2[:, cols], bank[:])
                else:
                    nc.vector.tensor_copy(h2[:, cols], bank[:])
                nc.scalar.activation(ds2[:].indirect(n6_list[:, cols.start // 16 : cols.stop // 16]), h2[:, cols], ACT.Copy)
                nc.scalar.activation(ds3[:].indirect(n7_list[:, cols.start // 16 : cols.stop // 16]), h2[:, cols], ACT.Copy)
            for cols in halves if m == TILES - 1 else whole:
                nc.scalar.activation(
                    sg[:, cols],
                    ds2[:].indirect(n8_list[:, cols.start // 16 : cols.stop // 16]),
                    ACT.Sigmoid,
                    bias=bias[:, m : m + 1],
                    scale=slope[:, m : m + 1],
                )
                nc.vector.tensor_tensor(result[:, cols], ds3[:, cols], sg[:, cols], ALU.mult)
                nc.sync.dma_start(out[m * P : (m + 1) * P, cols], result[:, cols])
